import numpy as np
import ml_dtypes


def mxq(x, axis, fmt="e4m3"):
    dtype, down = {"e4m3": (ml_dtypes.float8_e4m3fn, 7), "e5m2": (ml_dtypes.float8_e5m2, 14)}[fmt]
    v = np.moveaxis(np.asarray(x, np.float32).astype(ml_dtypes.bfloat16).astype(np.float64), axis, -1)
    blocks = v.reshape(v.shape[:-1] + (-1, 32))
    amax = np.abs(blocks).max(-1, keepdims=True)
    byte = np.maximum(np.where(amax > 0, np.frexp(amax)[1] - 1 + 127, 0) - down, 1)
    scale = np.exp2(byte - 127.0)
    codes = (blocks / scale).astype(np.float32).astype(dtype).astype(np.float64)
    return np.moveaxis((codes * scale).reshape(v.shape), -1, axis)


WIDE = False


def mx_kscale(k):
    if not WIDE:
        return np.ones(k)
    levels = np.array([10, -10, 5, -5, 0])
    if k % 512:
        return np.exp2(np.random.permutation(np.resize(levels, k // 32))).repeat(32)
    a = np.empty((k // 512, 16))
    for p in range(k // 512):
        a[p, :8] = np.random.permutation(np.resize(levels, 8))
        for g in range(8):
            far = levels[np.abs(levels - a[p, g]) >= 10]
            a[p, g + 8] = far[np.random.randint(len(far))]
    return np.exp2(a.ravel()).repeat(32)


def f64(x):
    return np.asarray(x).astype(np.float64)


def striped(idx):
    return np.tile(idx.reshape(-1, 16).T, (8, 1)).astype(np.uint16)


def unstriped(offs):
    return offs[:16].T.reshape(-1).astype(np.int64)


def striped8(idx):
    return np.concatenate([x.reshape(-1, 16).T for x in idx]).astype(np.uint16)


def runs(offs, k):
    lists = np.stack([offs[16 * r : 16 * r + 16].T.reshape(-1) for r in range(8)]).astype(np.int64)
    return lists[np.arange(k) % 512 // 64]


def pack_weight(w):
    k, n = w.shape
    w = f64(np.asarray(w, np.float32).astype(ml_dtypes.bfloat16)).reshape(k // 32, 32, n)
    amax = np.abs(w).max(1)
    byte = np.clip(np.where(amax > 0, np.frexp(amax)[1] - 1 + 127 - 7, 1), 1, 254)
    scaled = (w * np.exp2(127.0 - byte)[:, None, :]).reshape(k, n).astype(np.float32)
    words = np.ascontiguousarray(scaled.reshape(k // 512, 128, 4, n).transpose(0, 1, 3, 2)).astype(ml_dtypes.float8_e4m3fn).view(np.uint8)
    return words, np.ascontiguousarray(byte.astype(np.uint8).reshape(k // 512, 16, n))


def unpack_weight(words, scales):
    g, p, n, _ = words.shape
    vals = np.ascontiguousarray(words).view(ml_dtypes.float8_e4m3fn).astype(np.float64) * np.repeat(np.exp2(scales.astype(np.float64) - 127.0), 8, axis=1)[..., None]
    return vals.transpose(0, 1, 3, 2).reshape(g * 512, n)


def sigmoid(v):
    return 1.0 / (1.0 + np.exp(-np.maximum(v, -700.0)))


K, T, S, V, H, C, J = 512, 2048, 1024, 512, 512, 512, 512


def setup_inputs():
    n = np.random.standard_normal
    s = mx_kscale(K)[:, None]
    packed_xT = pack_weight(n((K, T)) * s)
    return {
        "x_words": packed_xT[0],
        "x_scales": packed_xT[1],
        "w1": (n((K, H)) / np.sqrt(K) / s).astype(np.float32),
        "gs": (np.random.uniform(0.5, 1.5, (K, 1)) / s).astype(np.float32),
        "tab": n((C, J)).astype(np.float32),
        "offs": striped(np.random.permutation(T)[:S]),
        "n1": striped8(np.stack([np.random.permutation(S) for _ in range(8)])),
        "cand": striped(np.random.permutation(T)[:C]),
        "n2": striped8(np.random.randint(0, J, (8, V))),
        "n3": striped8(np.stack([np.random.permutation(V) for _ in range(8)])),
    }


def reference(x_words, x_scales, w1, gs, tab, offs, n1, cand, n2, n3):
    x_cand = unpack_weight(x_words, x_scales)[:, unstriped(cand)]
    xq = unpack_weight(x_words, x_scales)[:, unstriped(offs)]
    y = mxq(f64(w1), 0, "e4m3").T @ xq
    ln = y[np.arange(H)[:, None], runs(n1, H)]
    mx = ln.reshape(H, V, 2).max(axis=2)
    mn = ln.reshape(H, V, 2).min(axis=2)
    z = f64(gs) * (mx * sigmoid(mn))
    s = 0.0625 * ((x_cand.T @ mxq(z, 0, "e4m3")))
    return np.maximum(s + f64(tab)[np.arange(C)[:, None], runs(n2, C)], s[np.arange(C)[:, None], runs(n3, C)])

from contextlib import ExitStack

import concourse.mybir as mybir
from concourse.masks import make_identity

K, T, S, V, H, C, J = 512, 2048, 1024, 512, 512, 512, 512
FLOPS = 2 * K * H * S + 2 * K * C * V

F32 = mybir.dt.float32
BF16 = mybir.dt.bfloat16
I32 = mybir.dt.int32
U32 = mybir.dt.uint32
U16 = mybir.dt.uint16
U8 = mybir.dt.uint8
FP8X4 = mybir.dt.float8_e4m3fn_x4
ALU = mybir.AluOpType
ACT = mybir.ActivationFunctionType

P = 128
PACK = 4
HALF = 256


def tile_picked_candpgatekind_none_p_kernel(tc, x_words, x_scales, w1, gs, tab, offs, n1, cand, n2, n3, out):
    nc = tc.nc
    with ExitStack() as ctx:
        keep = ctx.enter_context(tc.tile_pool(name="keep", bufs=1))
        ring = ctx.enter_context(tc.tile_pool(name="ring", bufs=2))
        mm = ctx.enter_context(tc.psum_pool(name="mm", bufs=4))
        tp = ctx.enter_context(tc.psum_pool(name="tp", bufs=2))

        offs_t = keep.tile([P, S // 16], U16, name="offs_t")
        n1_t = keep.tile([P, S // 16], U16, name="n1_t")
        cand_t = keep.tile([P, C // 16], U16, name="cand_t")
        n2_t = keep.tile([P, V // 16], U16, name="n2_t")
        n3_t = keep.tile([P, V // 16], U16, name="n3_t")
        xw = keep.tile([P, T], U32, name="xw")
        xs = keep.tile([P, T], U8, name="xs")
        w_raw = [keep.tile([P, PACK, HALF], F32, name="w_raw%d" % h) for h in range(2)]
        gs_t = keep.tile([P, PACK], F32, name="gs_t")
        tab_t = [keep.tile([P, J], F32, name="tab%d" % t) for t in range(PACK)]

        nc.gpsimd.memset(xs[:].bitcast(I32), 0)
        nc.sync.dma_start(offs_t[:], offs)
        for q in range(4):
            nc.sync.dma_start(xs[32 * q : 32 * q + 4, :].bitcast(I32), x_scales[0, 4 * q : 4 * q + 4, :].bitcast(I32))
        nc.sync.dma_start(cand_t[:], cand)
        w_rows = w1.rearrange("(p j) c -> p j c", j=PACK)
        for h in range(2):
            nc.sync.dma_start(w_raw[h][:], w_rows[:, :, h * HALF : (h + 1) * HALF])
        nc.sync.dma_start(xw[:].bitcast(I32), x_words[0].rearrange("p n r -> p (n r)").bitcast(I32))
        nc.sync.dma_start(n1_t[:], n1)
        nc.sync.dma_start(gs_t[:], gs.rearrange("(p t) o -> p (t o)", t=PACK))
        nc.sync.dma_start(n2_t[:], n2)
        nc.sync.dma_start(n3_t[:], n3)
        tab_rows = tab.rearrange("(p t) c -> p t c", t=PACK)
        for t in range(PACK):
            nc.sync.dma_start(tab_t[t][:], tab_rows[:, t, :])

        ident = keep.tile([P, P], F32, name="ident")
        make_identity(nc, ident[:])

        tok_b = keep.tile([P, S], U8, name="tok_b", align_bytes=64)
        nc.vector.tensor_copy(tok_b[:], xs[:].indirect(offs_t[:]))
        cand_b0 = keep.tile([P, C], U8, name="cand_b0", align_bytes=64)
        nc.vector.tensor_copy(cand_b0[:], xs[:].indirect(cand_t[:]))
        cand_b = keep.tile([P, PACK, P], U8, name="cand_b", align_bytes=64)
        nc.vector.tensor_copy(cand_b[:].rearrange("p t m -> p m t"), cand_b0[:].rearrange("p (m t) -> p m t", t=PACK))
        w_bf = keep.tile([P, PACK, P, PACK], BF16, name="w_bf", align_bytes=64)
        for h in range(2):
            nc.scalar.copy(
                w_bf[:, :, 64 * h : 64 * (h + 1), :].rearrange("p t m j -> p m t j"),
                w_raw[h][:].rearrange("p j (m t) -> p m t j", t=PACK),
            )
        w_codes = keep.tile([P, H], U32, name="w_codes", align_bytes=64)
        w_sc = keep.tile([P, H], U8, name="w_sc", align_bytes=64)
        nc.vector.quantize_mx(out=w_codes[:].bitcast(FP8X4), scales=w_sc[:], in_=w_bf[:].rearrange("p t m j -> p (t m j)"))

        tok_w = []
        for h in range(2):
            tw = keep.tile([P, 512], U32, name="tok_w%d" % h, align_bytes=64)
            nc.vector.tensor_copy(tw[:], xw[:].indirect(offs_t[:, 32 * h : 32 * (h + 1)]))
            tok_w.append(tw)

        y = []
        for t in range(PACK):
            yt = keep.tile([P, S], F32, name="y%d" % t)
            for h in range(2):
                acc = mm.tile([P, 512], F32, name="acc")
                nc.tensor.matmul_mx(
                    out=acc[:],
                    lhsT=w_codes[:, t * P : (t + 1) * P].bitcast(FP8X4),
                    lhsT_scale=w_sc[:, t * P : (t + 1) * P],
                    rhs=tok_w[h][:].bitcast(FP8X4),
                    rhs_scale=tok_b[:, 512 * h : 512 * (h + 1)],
                    start=True,
                    stop=True,
                )
                nc.scalar.copy(yt[:, 512 * h : 512 * (h + 1)], acc[:])
            y.append(yt)

        cand_w = keep.tile([P, PACK, P], U32, name="cand_w", align_bytes=64)
        nc.vector.tensor_copy(cand_w[:].rearrange("p t m -> p m t"), xw[:].indirect(cand_t[:]))

        s = [keep.tile([P, V], F32, name="s%d" % t) for t in range(PACK)]
        for h in range(2):
            zf = ring.tile([P, PACK, HALF], F32, name="zf")
            for u in range(2):
                ln = keep.tile([P, 2, 512], F32, name="ln", tag="ln%d" % u)
                for e in range(2):
                    nc.vector.tensor_copy(ln[:, e, :], y[2 * u + e][:].indirect(n1_t[:, 32 * h : 32 * (h + 1)]))
                pairs = ln[:].rearrange("p e (v two) -> p (e v) two", two=2)
                mn = ring.tile([P, 512], F32, name="mn")
                mx = ring.tile([P, 512], F32, name="mx")
                sg = keep.tile([P, 768], F32, name="sg", tag="sg%d" % u)
                nc.vector.tensor_tensor(mn[:], pairs[:, :, 0], pairs[:, :, 1], ALU.min)
                nc.vector.tensor_tensor(mx[:], pairs[:, :, 0], pairs[:, :, 1], ALU.max)
                nc.scalar.activation(sg[:, :512], mn[:], ACT.Sigmoid)
                for e in range(2):
                    t = 2 * u + e
                    cols = slice(e * HALF, (e + 1) * HALF)
                    nc.vector.scalar_tensor_tensor(zf[:, t, :], mx[:, cols], gs_t[:, t : t + 1], sg[:, cols], ALU.mult, ALU.mult)
            z_bf = keep.tile([P, HALF, PACK], BF16, name="z_bf", tag="zbf%d" % h, align_bytes=64)
            nc.scalar.copy(
                z_bf[:].rearrange("p (c i) t -> p c t i", i=4),
                zf[:].rearrange("p t (c i) -> p c t i", i=4),
            )
            z_codes = ring.tile([P, HALF], U32, name="z_codes", align_bytes=64)
            z_sc = ring.tile([P, HALF], U8, name="z_sc", align_bytes=64)
            nc.vector.quantize_mx(out=z_codes[:].bitcast(FP8X4), scales=z_sc[:], in_=z_bf[:].rearrange("p v t -> p (v t)"))
            for t in range(PACK):
                acc = mm.tile([P, 512], F32, name="acc")
                nc.tensor.matmul_mx(
                    out=acc[:, :HALF],
                    lhsT=cand_w[:, t, :].bitcast(FP8X4),
                    lhsT_scale=cand_b[:, t, :],
                    rhs=z_codes[:].bitcast(FP8X4),
                    rhs_scale=z_sc[:],
                    start=True,
                    stop=True,
                )
                nc.scalar.activation(s[t][:, h * HALF : (h + 1) * HALF], acc[:, :HALF], ACT.Copy, scale=0.0625)

        g_a = keep.tile([P, 1, HALF], F32, name="g_a", tag="ln1")
        g_b = keep.tile([P, 3, HALF], F32, name="g_b", tag="sg1")
        g_c = keep.tile([P, 4, HALF], F32, name="g_c", tag="zbf1", align_bytes=64)
        pieces = [g_a[:, 0, :]] + [g_b[:, i, :] for i in range(3)] + [g_c[:, i, :] for i in range(4)]
        for t in range(PACK):
            for h in range(2):
                nc.vector.tensor_copy(pieces[2 * t + h], tab_t[t][:].indirect(n2_t[:, 16 * h : 16 * (h + 1)]))

        out_rows = out.rearrange("(p t) v -> p t v", t=PACK)
        for t in range(PACK):
            s3 = ring.tile([P, V], F32, name="s3")
            for h in range(2):
                nc.vector.tensor_copy(s3[:, h * HALF : (h + 1) * HALF], s[t][:].indirect(n3_t[:, 16 * h : 16 * (h + 1)]))
            at_ps = tp.tile([P, V], F32, name="at_ps")
            for b in range(4):
                cols = slice(b * P, (b + 1) * P)
                nc.tensor.matmul(at_ps[:, cols], pieces[2 * t + b // 2][:, (b % 2) * P : (b % 2 + 1) * P], ident[:], is_transpose=True, start=True, stop=False)
                nc.tensor.matmul(at_ps[:, cols], s[t][:, cols], ident[:], is_transpose=True, start=False, stop=True)
            at_sb = ring.tile([P, V], F32, name="at_sb")
            nc.scalar.copy(at_sb[:], at_ps[:])
            a_ps = tp.tile([P, V], F32, name="a_ps")
            for b in range(4):
                cols = slice(b * P, (b + 1) * P)
                nc.tensor.transpose(a_ps[:, cols], at_sb[:, cols], ident[:])
            res = keep.tile([P, V], F32, name="res%d" % t)
            for cols in [slice(0, V)] if t < PACK - 1 else [slice(0, 384), slice(384, V)]:
                nc.vector.tensor_tensor(res[:, cols], a_ps[:, cols], s3[:, cols], ALU.max)
                nc.sync.dma_start(out_rows[:, t, cols], res[:, cols])
